import numpy as np
import ml_dtypes


def mxq(x, axis, fmt="e4m3"):
    dtype, down = {"e4m3": (ml_dtypes.float8_e4m3fn, 7), "e5m2": (ml_dtypes.float8_e5m2, 14)}[fmt]
    v = np.moveaxis(np.asarray(x, np.float32).astype(ml_dtypes.bfloat16).astype(np.float64), axis, -1)
    blocks = v.reshape(v.shape[:-1] + (-1, 32))
    amax = np.abs(blocks).max(-1, keepdims=True)
    byte = np.maximum(np.where(amax > 0, np.frexp(amax)[1] - 1 + 127, 0) - down, 1)
    scale = np.exp2(byte - 127.0)
    codes = (blocks / scale).astype(np.float32).astype(dtype).astype(np.float64)
    return np.moveaxis((codes * scale).reshape(v.shape), -1, axis)


WIDE = False


def mx_kscale(k):
    if not WIDE:
        return np.ones(k)
    levels = np.array([30, -30])
    if k % 512:
        return np.exp2(np.random.permutation(np.resize(levels, k // 32))).repeat(32)
    a = np.empty((k // 512, 16))
    for p in range(k // 512):
        a[p, :8] = np.random.permutation(np.resize(levels, 8))
        for g in range(8):
            far = levels[np.abs(levels - a[p, g]) >= 10]
            a[p, g + 8] = far[np.random.randint(len(far))]
    return np.exp2(a.ravel()).repeat(32)


def f64(x):
    return np.asarray(x).astype(np.float64)


def striped(idx):
    return np.tile(np.asarray(idx).reshape(-1, 16).T, (8, 1)).astype(np.uint16)


def unstriped(offs):
    return offs[:16].T.reshape(-1).astype(np.int64)


def striped8(idx):
    return np.asarray(idx).reshape(8, -1, 16).transpose(0, 2, 1).reshape(128, -1).astype(np.uint16)


def unstriped8(offs):
    return offs.reshape(8, 16, -1).transpose(0, 2, 1).reshape(8, -1).astype(np.int64)


def pick8(x, idx, run):
    r = np.arange(len(x))
    return x[r[:, None], idx[r % (8 * run) // run]]


E2M1 = np.array([0.0, 0.5, 1.0, 1.5, 2.0, 3.0, 4.0, 6.0, -0.0, -0.5, -1.0, -1.5, -2.0, -3.0, -4.0, -6.0])


def pack_weight(w, fmt):
    k, n = w.shape
    w = f64(np.asarray(w, np.float32).astype(ml_dtypes.bfloat16)).reshape(k // 32, 32, n)
    amax = np.abs(w).max(1)
    if fmt in ("e4m3", "e5m2"):
        byte = np.frexp(amax)[1] - 1 + 127 - (7 if fmt == "e4m3" else 14)
    else:
        mant, ex = np.frexp(amax / 6.0)
        byte = np.where(mant > 0.5, ex, ex - 1) + 127
    byte = np.clip(np.where(amax > 0, byte, 1), 1, 254)
    scaled = (w * np.exp2(127.0 - byte)[:, None, :]).reshape(k, n).astype(np.float32)
    by_word = np.ascontiguousarray(scaled.reshape(k // 512, 128, 4, n).transpose(0, 1, 3, 2))
    if fmt in ("e4m3", "e5m2"):
        words = by_word.astype(ml_dtypes.float8_e4m3fn if fmt == "e4m3" else ml_dtypes.float8_e5m2).view(np.uint8)
    else:
        c = by_word.astype(ml_dtypes.float4_e2m1fn).view(np.uint8) & 0xF
        words = (c[..., 0::2] | (c[..., 1::2] << 4)).reshape(k // 512, 128, 2 * n)
    return np.ascontiguousarray(words), np.ascontiguousarray(byte.astype(np.uint8).reshape(k // 512, 16, n))


def unpack_weight(words, scales, fmt):
    g, _, n = scales.shape
    words = np.ascontiguousarray(words).reshape(g, 128, n, -1)
    if fmt in ("e4m3", "e5m2"):
        vals = words.view(ml_dtypes.float8_e4m3fn if fmt == "e4m3" else ml_dtypes.float8_e5m2).astype(np.float64)
    else:
        nib = np.empty((g, 128, n, 4), np.uint8)
        nib[..., 0::2] = words & 0xF
        nib[..., 1::2] = words >> 4
        vals = E2M1[nib]
    vals = vals * np.repeat(np.exp2(scales.astype(np.float64) - 127.0), 8, axis=1)[..., None]
    return vals.transpose(0, 1, 3, 2).reshape(g * 512, n)


def sgn(shape):
    return np.random.uniform(0.5, 2.0, shape) * np.where(np.random.standard_normal(shape) < 0, -1.0, 1.0)


K, T, F, Z, J, N, E = 512, 512, 512, 1024, 256, 256, 512


def setup_inputs():
    n = np.random.standard_normal
    idx = np.stack([np.random.permutation(T)[:J] for _ in range(8)])
    idx2 = np.random.permutation(Z)[:J]
    idx3 = np.random.permutation(E)[:J]
    fk = mx_kscale(K)
    ff = mx_kscale(F)
    xop = pack_weight(n((F, Z)) / ff[:, None], "e5m2")
    wp = pack_weight(n((K, N)) * 1 / np.sqrt(K) / fk[:, None], "e5m2")
    w2p = pack_weight(n((F, N)) * 1 / np.sqrt(F) * ff[:, None], "e4m3")
    return {
        "ca": (np.random.randint(-7, 8, (K, T)).astype(np.float64)).astype(np.float32),
        "sa": (np.random.uniform(0.08, 0.3, (K, 1)) * fk[:, None]).astype(np.float32),
        "xo_words": xop[0],
        "xo_scales": xop[1],
        "w_words": wp[0],
        "w_scales": wp[1],
        "w2_words": w2p[0],
        "w2_scales": w2p[1],
        "so": (sgn((N, 1))).astype(np.float32),
        "offs": striped8(idx),
        "offs2": striped(idx2),
        "offs3": striped(idx3),
    }


def reference(ca, sa, xo_words, xo_scales, w_words, w_scales, w2_words, w2_scales, so, offs, offs2, offs3):
    idx = unstriped8(offs)
    idx2 = unstriped(offs2)
    idx3 = unstriped(offs3)
    xou = unpack_weight(xo_words, xo_scales, "e5m2")
    wu = unpack_weight(w_words, w_scales, "e5m2")
    w2u = unpack_weight(w2_words, w2_scales, "e4m3")
    z1 = pick8(f64(ca), idx, 64) * f64(sa)
    z1q = mxq(z1, 0, "e4m3")
    xoidx2g = xou[:, idx2]
    p = wu.T @ z1q + w2u.T @ xoidx2g
    y = np.zeros((N, E))
    y[:, idx3] = p * f64(so)
    return y

@@ -1,0 +1,160 @@
+from contextlib import ExitStack
+
+import concourse.mybir as mybir
+
+F32 = mybir.dt.float32
+BF16 = mybir.dt.bfloat16
+I32 = mybir.dt.int32
+U32 = mybir.dt.uint32
+U16 = mybir.dt.uint16
+U8 = mybir.dt.uint8
+E4M3 = mybir.dt.float8_e4m3fn_x4
+E5M2 = mybir.dt.float8_e5m2_x4
+COPY = mybir.ActivationFunctionType.Copy
+
+P = 128
+PACK = 4
+K, T, F, Z, J, N, E = 512, 512, 512, 1024, 256, 256, 512
+HALF = J // 2
+N_TILES = N // P
+
+FLOPS = 2 * (K + F) * N * J
+
+
+def entries(list_tile, cases):
+    return list_tile[:, cases.start // 16 : cases.stop // 16]
+
+
+def tile_list_codesbeside_kernel(tc, ca, sa, xo_words, xo_scales, w_words, w_scales, w2_words, w2_scales, so, offs, offs2, offs3, out):
+    nc = tc.nc
+    halves = (slice(0, HALF), slice(HALF, J))
+    every = slice(0, J)
+    with ExitStack() as ctx:
+        sb = ctx.enter_context(tc.tile_pool(name="sb", bufs=1))
+        ps = ctx.enter_context(tc.psum_pool(name="ps", bufs=1))
+
+        code_list = sb.tile([P, J // 16], U16, name="code_list")
+        token_list = sb.tile([P, J // 16], U16, name="token_list")
+        page_list = sb.tile([P, J // 16], U16, name="page_list")
+        step = sb.tile([P, PACK], F32, name="step")
+        weight = sb.tile([P, N_TILES], F32, name="weight")
+        table = [sb.tile([P, T], F32, name="table%d" % r) for r in range(PACK)]
+        tokens = sb.tile([P, Z], I32, name="tokens")
+        w_tile = sb.tile([P, N], I32, name="w_tile", align_bytes=64)
+        w2_tile = sb.tile([P, N], I32, name="w2_tile", align_bytes=64)
+        token_stage = sb.tile([P, 2 * Z // 4], I32, name="token_stage")
+        w_stage = sb.tile([4, N], I32, name="w_stage")
+        w2_stage = sb.tile([4, N], I32, name="w2_stage", tag="stage_then_codes", align_bytes=64)
+        token_plane = sb.tile([P, Z], U8, name="token_plane")
+        w_plane = sb.tile([P, N], U8, name="w_plane", align_bytes=64)
+        w2_plane = sb.tile([P, N], U8, name="w2_plane", align_bytes=64)
+        page = [sb.tile([P, E], F32, name="page%d" % t) for t in range(N_TILES)]
+
+        ca_rows = ca.rearrange("(p r) t -> p r t", r=PACK)
+
+        def words(src):
+            return src[0].rearrange("p n b -> p (n b)").bitcast(I32)
+
+        def scale_rows(scales):
+            return scales[0].rearrange("(q r) c -> r q c", r=4).bitcast(I32)
+
+        for u in range(2):
+            nc.scalar.dma_start(
+                token_stage[64 * u : 64 * u + 4, :].rearrange("r (q c) -> r q c", q=2),
+                scale_rows(xo_scales)[:, 2 * u : 2 * u + 2, :],
+            )
+        nc.sync.dma_start(table[0][:], ca_rows[:, 0, :])
+        nc.sync.dma_start(code_list[:], offs)
+        nc.sync.dma_start(token_list[:], offs2)
+        nc.sync.dma_start(step[:], sa.rearrange("(p r) o -> p (r o)", r=PACK))
+        for r in range(1, PACK):
+            nc.sync.dma_start(table[r][:], ca_rows[:, r, :])
+        for stage, scales in ((w_stage, w_scales), (w2_stage, w2_scales)):
+            nc.sync.dma_start(stage[:].rearrange("r (q c) -> r q c", q=4), scale_rows(scales))
+        nc.sync.dma_start(tokens[:], words(xo_words))
+        nc.sync.dma_start(w_tile[:], words(w_words))
+        nc.sync.dma_start(w2_tile[:], words(w2_words))
+        nc.sync.dma_start(page_list[:], offs3)
+        with nc.allow_non_contiguous_dma(reason="one weight for each output feature, features on partitions"):
+            nc.sync.dma_start(weight[:], so.rearrange("(t p) o -> p (t o)", p=P))
+
+        idle_in = sb.tile([P, 1], F32, name="idle_in")
+        idle_out = sb.tile([P, 1], F32, name="idle_out")
+        nc.vector.memset(idle_in[:], 0.0)
+        nc.scalar.activation(idle_out[:], idle_in[:], COPY)
+
+        for plane in (token_plane, w_plane, w2_plane):
+            nc.vector.memset(plane[:].bitcast(I32), 0)
+        for t in range(N_TILES):
+            nc.vector.memset(page[t][:], 0.0)
+
+        width = Z // 4
+        for q in range(4):
+            src = 64 * (q // 2)
+            nc.vector.tensor_copy(
+                token_plane[32 * q : 32 * q + 4, :].bitcast(I32),
+                token_stage[src : src + 4, width * (q % 2) : width * (q % 2 + 1)],
+            )
+        picked_plane = sb.tile([P, J], U8, name="picked_plane", align_bytes=64)
+        nc.vector.tensor_copy(picked_plane[:], token_plane[:].indirect(token_list[:]))
+        width = N // 4
+        for plane, stage in ((w_plane, w_stage), (w2_plane, w2_stage)):
+            for q in range(4):
+                nc.vector.tensor_copy(
+                    plane[32 * q : 32 * q + 4, :].bitcast(I32),
+                    stage[0:4, width * q : width * (q + 1)],
+                )
+
+        z = sb.tile([P, PACK * J], BF16, name="z", align_bytes=64)
+        for r in range(PACK):
+            for cases in halves if r == PACK - 1 else (every,):
+                nc.scalar.activation(
+                    z[:, PACK * cases.start + r : PACK * cases.stop : PACK],
+                    table[r][:].indirect(entries(code_list, cases)),
+                    COPY,
+                    scale=step[:, r : r + 1],
+                )
+
+        z_words = sb.tile([P, J], U32, name="z_words", tag="stage_then_codes", align_bytes=64)
+        z_plane = sb.tile([P, J], U8, name="z_plane", align_bytes=64)
+        picked = sb.tile([P, J], U32, name="picked", align_bytes=64)
+        for cases in halves:
+            nc.vector.quantize_mx(
+                z_words[:, cases].bitcast(E4M3),
+                z_plane[:, cases],
+                z[:, PACK * cases.start : PACK * cases.stop],
+            )
+            nc.vector.tensor_copy(picked[:, cases], tokens[:].bitcast(U32).indirect(entries(token_list, cases)))
+
+        for u, (t, cases) in enumerate(((0, halves[0]), (1, every), (0, halves[1]))):
+            cols = slice(P * t, P * (t + 1))
+            count = cases.stop - cases.start
+            acc = ps.tile([P, count], F32, name="acc%d" % u)
+            nc.tensor.matmul_mx(
+                acc[:],
+                lhsT=w_tile[:, cols].bitcast(E5M2),
+                lhsT_scale=w_plane[:, cols],
+                rhs=z_words[:, cases].bitcast(E4M3),
+                rhs_scale=z_plane[:, cases],
+                start=True,
+                stop=False,
+            )
+            nc.tensor.matmul_mx(
+                acc[:],
+                lhsT=w2_tile[:, cols].bitcast(E4M3),
+                lhsT_scale=w2_plane[:, cols],
+                rhs=picked[:, cases].bitcast(E5M2),
+                rhs_scale=picked_plane[:, cases],
+                start=False,
+                stop=True,
+            )
+            sums = sb.tile([P, count], F32, name="sums%d" % u)
+            nc.vector.tensor_copy(sums[:], acc[:])
+            nc.scalar.activation(
+                page[t][:].indirect(entries(page_list, cases)),
+                sums[:],
+                COPY,
+                scale=weight[:, t : t + 1],
+            )
+        for t in reversed(range(N_TILES)):
+            nc.sync.dma_start(out[P * t : P * (t + 1), :], page[t][:])

@@ -37,18 +37,17 @@ def tile_list_codesbeside_kernel(tc, ca, sa, xo_words, xo_scales, w_words, w_sca
         token_list = sb.tile([P, J // 16], U16, name="token_list")
         page_list = sb.tile([P, J // 16], U16, name="page_list")
         step = sb.tile([P, PACK], F32, name="step")
-        weight = sb.tile([P, N_TILES], F32, name="weight")
+        weight = [sb.tile([P, 1], F32, name="weight%d" % t) for t in range(N_TILES)]
         table = [sb.tile([P, T], F32, name="table%d" % r) for r in range(PACK)]
         tokens = sb.tile([P, Z], I32, name="tokens")
         w_tile = sb.tile([P, N], I32, name="w_tile", align_bytes=64)
         w2_tile = sb.tile([P, N], I32, name="w2_tile", align_bytes=64)
-        token_stage = sb.tile([P, 2 * Z // 4], I32, name="token_stage")
-        w_stage = sb.tile([4, N], I32, name="w_stage")
-        w2_stage = sb.tile([4, N], I32, name="w2_stage", tag="stage_then_codes", align_bytes=64)
-        token_plane = sb.tile([P, Z], U8, name="token_plane")
+        token_stage = sb.tile([P, 2 * Z // 4], I32, name="token_stage", tag="stage_then_codes", align_bytes=64)
+        w_stage = sb.tile([4, N], I32, name="w_stage", tag="stage_then_page0")
+        w2_stage = sb.tile([4, N], I32, name="w2_stage", tag="stage_then_page1")
+        token_plane = sb.tile([P, Z], U8, name="token_plane", tag="plane_then_picked", align_bytes=64)
         w_plane = sb.tile([P, N], U8, name="w_plane", align_bytes=64)
         w2_plane = sb.tile([P, N], U8, name="w2_plane", align_bytes=64)
-        page = [sb.tile([P, E], F32, name="page%d" % t) for t in range(N_TILES)]
 
         ca_rows = ca.rearrange("(p r) t -> p r t", r=PACK)
 
@@ -59,24 +58,25 @@ def tile_list_codesbeside_kernel(tc, ca, sa, xo_words, xo_scales, w_words, w_sca
             return scales[0].rearrange("(q r) c -> r q c", r=4).bitcast(I32)
 
         for u in range(2):
-            nc.scalar.dma_start(
+            nc.gpsimd.dma_start(
                 token_stage[64 * u : 64 * u + 4, :].rearrange("r (q c) -> r q c", q=2),
                 scale_rows(xo_scales)[:, 2 * u : 2 * u + 2, :],
             )
+        for stage, scales in ((w_stage, w_scales), (w2_stage, w2_scales)):
+            nc.scalar.dma_start(stage[:].rearrange("r (q c) -> r q c", q=4), scale_rows(scales))
         nc.sync.dma_start(table[0][:], ca_rows[:, 0, :])
         nc.sync.dma_start(code_list[:], offs)
-        nc.sync.dma_start(token_list[:], offs2)
         nc.sync.dma_start(step[:], sa.rearrange("(p r) o -> p (r o)", r=PACK))
-        for r in range(1, PACK):
-            nc.sync.dma_start(table[r][:], ca_rows[:, r, :])
-        for stage, scales in ((w_stage, w_scales), (w2_stage, w2_scales)):
-            nc.sync.dma_start(stage[:].rearrange("r (q c) -> r q c", q=4), scale_rows(scales))
+        nc.sync.dma_start(table[1][:], ca_rows[:, 1, :])
+        nc.sync.dma_start(token_list[:], offs2)
+        nc.sync.dma_start(table[2][:], ca_rows[:, 2, :])
+        nc.sync.dma_start(table[3][:], ca_rows[:, 3, :])
         nc.sync.dma_start(tokens[:], words(xo_words))
         nc.sync.dma_start(w_tile[:], words(w_words))
         nc.sync.dma_start(w2_tile[:], words(w2_words))
         nc.sync.dma_start(page_list[:], offs3)
-        with nc.allow_non_contiguous_dma(reason="one weight for each output feature, features on partitions"):
-            nc.sync.dma_start(weight[:], so.rearrange("(t p) o -> p (t o)", p=P))
+        for t in range(N_TILES):
+            nc.sync.dma_start(weight[t][:], so[P * t : P * (t + 1), :])
 
         idle_in = sb.tile([P, 1], F32, name="idle_in")
         idle_out = sb.tile([P, 1], F32, name="idle_out")
@@ -85,9 +85,17 @@ def tile_list_codesbeside_kernel(tc, ca, sa, xo_words, xo_scales, w_words, w_sca
 
         for plane in (token_plane, w_plane, w2_plane):
             nc.vector.memset(plane[:].bitcast(I32), 0)
+
+        width = N // 4
+        for plane, stage in ((w_plane, w_stage), (w2_plane, w2_stage)):
+            for q in range(4):
+                nc.vector.tensor_copy(
+                    plane[32 * q : 32 * q + 4, :].bitcast(I32),
+                    stage[0:4, width * q : width * (q + 1)],
+                )
+        page = [sb.tile([P, E], F32, name="page%d" % t, tag="stage_then_page%d" % t) for t in range(N_TILES)]
         for t in range(N_TILES):
             nc.vector.memset(page[t][:], 0.0)
-
         width = Z // 4
         for q in range(4):
             src = 64 * (q // 2)
@@ -97,13 +105,6 @@ def tile_list_codesbeside_kernel(tc, ca, sa, xo_words, xo_scales, w_words, w_sca
             )
         picked_plane = sb.tile([P, J], U8, name="picked_plane", align_bytes=64)
         nc.vector.tensor_copy(picked_plane[:], token_plane[:].indirect(token_list[:]))
-        width = N // 4
-        for plane, stage in ((w_plane, w_stage), (w2_plane, w2_stage)):
-            for q in range(4):
-                nc.vector.tensor_copy(
-                    plane[32 * q : 32 * q + 4, :].bitcast(I32),
-                    stage[0:4, width * q : width * (q + 1)],
-                )
 
         z = sb.tile([P, PACK * J], BF16, name="z", align_bytes=64)
         for r in range(PACK):
@@ -117,13 +118,14 @@ def tile_list_codesbeside_kernel(tc, ca, sa, xo_words, xo_scales, w_words, w_sca
 
         z_words = sb.tile([P, J], U32, name="z_words", tag="stage_then_codes", align_bytes=64)
         z_plane = sb.tile([P, J], U8, name="z_plane", align_bytes=64)
-        picked = sb.tile([P, J], U32, name="picked", align_bytes=64)
+        picked = sb.tile([P, J], U32, name="picked", tag="plane_then_picked", align_bytes=64)
         for cases in halves:
             nc.vector.quantize_mx(
                 z_words[:, cases].bitcast(E4M3),
                 z_plane[:, cases],
                 z[:, PACK * cases.start : PACK * cases.stop],
             )
+        for cases in halves:
             nc.vector.tensor_copy(picked[:, cases], tokens[:].bitcast(U32).indirect(entries(token_list, cases)))
 
         for u, (t, cases) in enumerate(((0, halves[0]), (1, every), (0, halves[1]))):
@@ -132,19 +134,19 @@ def tile_list_codesbeside_kernel(tc, ca, sa, xo_words, xo_scales, w_words, w_sca
             acc = ps.tile([P, count], F32, name="acc%d" % u)
             nc.tensor.matmul_mx(
                 acc[:],
-                lhsT=w_tile[:, cols].bitcast(E5M2),
-                lhsT_scale=w_plane[:, cols],
-                rhs=z_words[:, cases].bitcast(E4M3),
-                rhs_scale=z_plane[:, cases],
+                lhsT=w2_tile[:, cols].bitcast(E4M3),
+                lhsT_scale=w2_plane[:, cols],
+                rhs=picked[:, cases].bitcast(E5M2),
+                rhs_scale=picked_plane[:, cases],
                 start=True,
                 stop=False,
             )
             nc.tensor.matmul_mx(
                 acc[:],
-                lhsT=w2_tile[:, cols].bitcast(E4M3),
-                lhsT_scale=w2_plane[:, cols],
-                rhs=picked[:, cases].bitcast(E5M2),
-                rhs_scale=picked_plane[:, cases],
+                lhsT=w_tile[:, cols].bitcast(E5M2),
+                lhsT_scale=w_plane[:, cols],
+                rhs=z_words[:, cases].bitcast(E4M3),
+                rhs_scale=z_plane[:, cases],
                 start=False,
                 stop=True,
             )
@@ -154,7 +156,7 @@ def tile_list_codesbeside_kernel(tc, ca, sa, xo_words, xo_scales, w_words, w_sca
                 page[t][:].indirect(entries(page_list, cases)),
                 sums[:],
                 COPY,
-                scale=weight[:, t : t + 1],
+                scale=weight[t][:],
             )
         for t in reversed(range(N_TILES)):
             nc.sync.dma_start(out[P * t : P * (t + 1), :], page[t][:])

@@ -40,43 +40,45 @@ def tile_list_codesbeside_kernel(tc, ca, sa, xo_words, xo_scales, w_words, w_sca
         weight = [sb.tile([P, 1], F32, name="weight%d" % t) for t in range(N_TILES)]
         table = [sb.tile([P, T], F32, name="table%d" % r) for r in range(PACK)]
         tokens = sb.tile([P, Z], I32, name="tokens")
-        w_tile = sb.tile([P, N], I32, name="w_tile", align_bytes=64)
-        w2_tile = sb.tile([P, N], I32, name="w2_tile", align_bytes=64)
-        token_stage = sb.tile([P, 2 * Z // 4], I32, name="token_stage", tag="stage_then_codes", align_bytes=64)
-        w_stage = sb.tile([4, N], I32, name="w_stage", tag="stage_then_page0")
-        w2_stage = sb.tile([4, N], I32, name="w2_stage", tag="stage_then_page1")
-        token_plane = sb.tile([P, Z], U8, name="token_plane", tag="plane_then_picked", align_bytes=64)
+        w_tile = [sb.tile([P, P], I32, name="w_tile%d" % t, align_bytes=64) for t in range(N_TILES)]
+        w2_tile = [sb.tile([P, P], I32, name="w2_tile%d" % t, align_bytes=64) for t in range(N_TILES)]
+        token_stage = sb.tile([4, Z], I32, name="token_stage")
+        w_stage = sb.tile([4, N], I32, name="w_stage")
+        w2_stage = sb.tile([4, N], I32, name="w2_stage", tag="stage_then_codes", align_bytes=64)
+        token_plane = sb.tile([P, Z], U8, name="token_plane")
         w_plane = sb.tile([P, N], U8, name="w_plane", align_bytes=64)
         w2_plane = sb.tile([P, N], U8, name="w2_plane", align_bytes=64)
+        page = [sb.tile([P, E], F32, name="page%d" % t) for t in range(N_TILES)]
 
         ca_rows = ca.rearrange("(p r) t -> p r t", r=PACK)
 
-        def words(src):
-            return src[0].rearrange("p n b -> p (n b)").bitcast(I32)
+        def words(src, t):
+            return src[0].rearrange("p n b -> p (n b)")[:, 4 * P * t : 4 * P * (t + 1)].bitcast(I32)
 
         def scale_rows(scales):
             return scales[0].rearrange("(q r) c -> r q c", r=4).bitcast(I32)
 
-        for u in range(2):
-            nc.gpsimd.dma_start(
-                token_stage[64 * u : 64 * u + 4, :].rearrange("r (q c) -> r q c", q=2),
-                scale_rows(xo_scales)[:, 2 * u : 2 * u + 2, :],
-            )
-        for stage, scales in ((w_stage, w_scales), (w2_stage, w2_scales)):
-            nc.scalar.dma_start(stage[:].rearrange("r (q c) -> r q c", q=4), scale_rows(scales))
+        def load_stage(stage, scales):
+            nc.sync.dma_start(stage[:].rearrange("r (q c) -> r q c", q=4), scale_rows(scales))
+
+        nc.scalar.dma_start(step[:], sa.rearrange("(p r) o -> p (r o)", r=PACK))
         nc.sync.dma_start(table[0][:], ca_rows[:, 0, :])
         nc.sync.dma_start(code_list[:], offs)
-        nc.sync.dma_start(step[:], sa.rearrange("(p r) o -> p (r o)", r=PACK))
         nc.sync.dma_start(table[1][:], ca_rows[:, 1, :])
         nc.sync.dma_start(token_list[:], offs2)
+        load_stage(token_stage, xo_scales)
         nc.sync.dma_start(table[2][:], ca_rows[:, 2, :])
+        load_stage(w_stage, w_scales)
+        load_stage(w2_stage, w2_scales)
         nc.sync.dma_start(table[3][:], ca_rows[:, 3, :])
-        nc.sync.dma_start(tokens[:], words(xo_words))
-        nc.sync.dma_start(w_tile[:], words(w_words))
-        nc.sync.dma_start(w2_tile[:], words(w2_words))
+        nc.sync.dma_start(tokens[:], xo_words[0].rearrange("p n b -> p (n b)").bitcast(I32))
+        nc.sync.dma_start(w_tile[0][:], words(w_words, 0))
+        nc.sync.dma_start(w2_tile[0][:], words(w2_words, 0))
         nc.sync.dma_start(page_list[:], offs3)
-        for t in range(N_TILES):
-            nc.sync.dma_start(weight[t][:], so[P * t : P * (t + 1), :])
+        nc.sync.dma_start(weight[0][:], so[0:P, :])
+        nc.sync.dma_start(w_tile[1][:], words(w_words, 1))
+        nc.sync.dma_start(w2_tile[1][:], words(w2_words, 1))
+        nc.sync.dma_start(weight[1][:], so[P:N, :])
 
         idle_in = sb.tile([P, 1], F32, name="idle_in")
         idle_out = sb.tile([P, 1], F32, name="idle_out")
@@ -85,26 +87,22 @@ def tile_list_codesbeside_kernel(tc, ca, sa, xo_words, xo_scales, w_words, w_sca
 
         for plane in (token_plane, w_plane, w2_plane):
             nc.vector.memset(plane[:].bitcast(I32), 0)
+        for t in range(N_TILES):
+            nc.vector.memset(page[t][:], 0.0)
 
-        width = N // 4
-        for plane, stage in ((w_plane, w_stage), (w2_plane, w2_stage)):
+        def spread(plane, stage):
+            width = stage.shape[1] // 4
             for q in range(4):
                 nc.vector.tensor_copy(
                     plane[32 * q : 32 * q + 4, :].bitcast(I32),
                     stage[0:4, width * q : width * (q + 1)],
                 )
-        page = [sb.tile([P, E], F32, name="page%d" % t, tag="stage_then_page%d" % t) for t in range(N_TILES)]
-        for t in range(N_TILES):
-            nc.vector.memset(page[t][:], 0.0)
-        width = Z // 4
-        for q in range(4):
-            src = 64 * (q // 2)
-            nc.vector.tensor_copy(
-                token_plane[32 * q : 32 * q + 4, :].bitcast(I32),
-                token_stage[src : src + 4, width * (q % 2) : width * (q % 2 + 1)],
-            )
+
+        spread(token_plane, token_stage)
         picked_plane = sb.tile([P, J], U8, name="picked_plane", align_bytes=64)
         nc.vector.tensor_copy(picked_plane[:], token_plane[:].indirect(token_list[:]))
+        spread(w_plane, w_stage)
+        spread(w2_plane, w2_stage)
 
         z = sb.tile([P, PACK * J], BF16, name="z", align_bytes=64)
         for r in range(PACK):
@@ -116,47 +114,64 @@ def tile_list_codesbeside_kernel(tc, ca, sa, xo_words, xo_scales, w_words, w_sca
                     scale=step[:, r : r + 1],
                 )
 
-        z_words = sb.tile([P, J], U32, name="z_words", tag="stage_then_codes", align_bytes=64)
-        z_plane = sb.tile([P, J], U8, name="z_plane", align_bytes=64)
-        picked = sb.tile([P, J], U32, name="picked", tag="plane_then_picked", align_bytes=64)
-        for cases in halves:
-            nc.vector.quantize_mx(
-                z_words[:, cases].bitcast(E4M3),
-                z_plane[:, cases],
-                z[:, PACK * cases.start : PACK * cases.stop],
-            )
-        for cases in halves:
-            nc.vector.tensor_copy(picked[:, cases], tokens[:].bitcast(U32).indirect(entries(token_list, cases)))
+        tags = ("stage_then_codes", "picked_then_codes")
+        picked = [
+            sb.tile([P, HALF], U32, name="picked0", tag=tags[1], align_bytes=64),
+            sb.tile([P, HALF], U32, name="picked1", align_bytes=64),
+        ]
 
-        for u, (t, cases) in enumerate(((0, halves[0]), (1, every), (0, halves[1]))):
-            cols = slice(P * t, P * (t + 1))
-            count = cases.stop - cases.start
-            acc = ps.tile([P, count], F32, name="acc%d" % u)
+        def quantise(h):
+            z_words = sb.tile([P, HALF], U32, name="z_words%d" % h, tag=tags[h], align_bytes=64)
+            z_plane = sb.tile([P, HALF], U8, name="z_plane%d" % h, align_bytes=64)
+            cases = halves[h]
+            nc.vector.quantize_mx(z_words[:].bitcast(E4M3), z_plane[:], z[:, PACK * cases.start : PACK * cases.stop])
+            return z_words, z_plane
+
+        def code_pass(acc, t, codes, first):
             nc.tensor.matmul_mx(
                 acc[:],
-                lhsT=w2_tile[:, cols].bitcast(E4M3),
-                lhsT_scale=w2_plane[:, cols],
-                rhs=picked[:, cases].bitcast(E5M2),
-                rhs_scale=picked_plane[:, cases],
-                start=True,
-                stop=False,
+                lhsT=w_tile[t][:].bitcast(E5M2),
+                lhsT_scale=w_plane[:, P * t : P * (t + 1)],
+                rhs=codes[0][:].bitcast(E4M3),
+                rhs_scale=codes[1][:],
+                start=first,
+                stop=not first,
             )
+
+        def token_pass(acc, t, h, first):
             nc.tensor.matmul_mx(
                 acc[:],
-                lhsT=w_tile[:, cols].bitcast(E5M2),
-                lhsT_scale=w_plane[:, cols],
-                rhs=z_words[:, cases].bitcast(E4M3),
-                rhs_scale=z_plane[:, cases],
-                start=False,
-                stop=True,
+                lhsT=w2_tile[t][:].bitcast(E4M3),
+                lhsT_scale=w2_plane[:, P * t : P * (t + 1)],
+                rhs=picked[h][:].bitcast(E5M2),
+                rhs_scale=picked_plane[:, halves[h]],
+                start=first,
+                stop=not first,
             )
-            sums = sb.tile([P, count], F32, name="sums%d" % u)
+
+        def put(acc, t, h):
+            sums = sb.tile([P, HALF], F32, name="sums%d%d" % (t, h))
             nc.vector.tensor_copy(sums[:], acc[:])
             nc.scalar.activation(
-                page[t][:].indirect(entries(page_list, cases)),
+                page[t][:].indirect(entries(page_list, halves[h])),
                 sums[:],
                 COPY,
                 scale=weight[t][:],
             )
-        for t in reversed(range(N_TILES)):
+
+        codes = quantise(0)
+        for h in range(2):
+            nc.vector.tensor_copy(picked[h][:], tokens[:].bitcast(U32).indirect(entries(token_list, halves[h])))
+        for t in range(N_TILES):
+            acc = ps.tile([P, HALF], F32, name="acc%d0" % t)
+            code_pass(acc, t, codes, True)
+            token_pass(acc, t, 0, False)
+            put(acc, t, 0)
+        codes = quantise(1)
+        for t in range(N_TILES):
+            acc = ps.tile([P, HALF], F32, name="acc%d1" % t)
+            token_pass(acc, t, 1, True)
+            code_pass(acc, t, codes, False)
+            put(acc, t, 1)
+        for t in range(N_TILES):
             nc.sync.dma_start(out[P * t : P * (t + 1), :], page[t][:])

@@ -1,6 +1,7 @@
 from contextlib import ExitStack
 
 import concourse.mybir as mybir
+from concourse.masks import make_identity
 
 F32 = mybir.dt.float32
 BF16 = mybir.dt.bfloat16
@@ -37,14 +38,16 @@ def tile_list_codesbeside_kernel(tc, ca, sa, xo_words, xo_scales, w_words, w_sca
         token_list = sb.tile([P, J // 16], U16, name="token_list")
         page_list = sb.tile([P, J // 16], U16, name="page_list")
         step = sb.tile([P, PACK], F32, name="step")
-        weight = [sb.tile([P, 1], F32, name="weight%d" % t) for t in range(N_TILES)]
+        weight_rows = sb.tile([P, P], F32, name="weight_rows")
+        identity = sb.tile([P, P], F32, name="identity")
+        weight = sb.tile([P, N_TILES], F32, name="weight")
         table = [sb.tile([P, T], F32, name="table%d" % r) for r in range(PACK)]
         tokens = sb.tile([P, Z], I32, name="tokens")
-        w_tile = [sb.tile([P, P], I32, name="w_tile%d" % t, align_bytes=64) for t in range(N_TILES)]
-        w2_tile = [sb.tile([P, P], I32, name="w2_tile%d" % t, align_bytes=64) for t in range(N_TILES)]
-        token_stage = sb.tile([4, Z], I32, name="token_stage")
+        w_tile = sb.tile([P, N], I32, name="w_tile", align_bytes=64)
+        w2_tile = sb.tile([P, N], I32, name="w2_tile", align_bytes=64)
+        token_stage = sb.tile([P, 2 * Z // 4], I32, name="token_stage")
         w_stage = sb.tile([4, N], I32, name="w_stage")
-        w2_stage = sb.tile([4, N], I32, name="w2_stage", tag="stage_then_codes", align_bytes=64)
+        w2_stage = sb.tile([4, N], I32, name="w2_stage")
         token_plane = sb.tile([P, Z], U8, name="token_plane")
         w_plane = sb.tile([P, N], U8, name="w_plane", align_bytes=64)
         w2_plane = sb.tile([P, N], U8, name="w2_plane", align_bytes=64)
@@ -52,33 +55,32 @@ def tile_list_codesbeside_kernel(tc, ca, sa, xo_words, xo_scales, w_words, w_sca
 
         ca_rows = ca.rearrange("(p r) t -> p r t", r=PACK)
 
-        def words(src, t):
-            return src[0].rearrange("p n b -> p (n b)")[:, 4 * P * t : 4 * P * (t + 1)].bitcast(I32)
+        def words(src):
+            return src[0].rearrange("p n b -> p (n b)").bitcast(I32)
 
         def scale_rows(scales):
             return scales[0].rearrange("(q r) c -> r q c", r=4).bitcast(I32)
 
-        def load_stage(stage, scales):
-            nc.sync.dma_start(stage[:].rearrange("r (q c) -> r q c", q=4), scale_rows(scales))
-
+        nc.vector.memset(weight_rows[:], 0.0)
         nc.scalar.dma_start(step[:], sa.rearrange("(p r) o -> p (r o)", r=PACK))
+        for u in range(2):
+            nc.sync.dma_start(
+                token_stage[64 * u : 64 * u + 4, :].rearrange("r (q c) -> r q c", q=2),
+                scale_rows(xo_scales)[:, 2 * u : 2 * u + 2, :],
+            )
+        for stage, scales in ((w_stage, w_scales), (w2_stage, w2_scales)):
+            nc.sync.dma_start(stage[:].rearrange("r (q c) -> r q c", q=4), scale_rows(scales))
         nc.sync.dma_start(table[0][:], ca_rows[:, 0, :])
         nc.sync.dma_start(code_list[:], offs)
         nc.sync.dma_start(table[1][:], ca_rows[:, 1, :])
-        nc.sync.dma_start(token_list[:], offs2)
-        load_stage(token_stage, xo_scales)
         nc.sync.dma_start(table[2][:], ca_rows[:, 2, :])
-        load_stage(w_stage, w_scales)
-        load_stage(w2_stage, w2_scales)
+        nc.sync.dma_start(token_list[:], offs2)
         nc.sync.dma_start(table[3][:], ca_rows[:, 3, :])
-        nc.sync.dma_start(tokens[:], xo_words[0].rearrange("p n b -> p (n b)").bitcast(I32))
-        nc.sync.dma_start(w_tile[0][:], words(w_words, 0))
-        nc.sync.dma_start(w2_tile[0][:], words(w2_words, 0))
+        nc.sync.dma_start(weight_rows[0:N_TILES, :], so.rearrange("(t p) o -> t (p o)", p=P))
+        nc.sync.dma_start(tokens[:], words(xo_words))
+        nc.sync.dma_start(w_tile[:], words(w_words))
+        nc.sync.dma_start(w2_tile[:], words(w2_words))
         nc.sync.dma_start(page_list[:], offs3)
-        nc.sync.dma_start(weight[0][:], so[0:P, :])
-        nc.sync.dma_start(w_tile[1][:], words(w_words, 1))
-        nc.sync.dma_start(w2_tile[1][:], words(w2_words, 1))
-        nc.sync.dma_start(weight[1][:], so[P:N, :])
 
         idle_in = sb.tile([P, 1], F32, name="idle_in")
         idle_out = sb.tile([P, 1], F32, name="idle_out")
@@ -98,11 +100,22 @@ def tile_list_codesbeside_kernel(tc, ca, sa, xo_words, xo_scales, w_words, w_sca
                     stage[0:4, width * q : width * (q + 1)],
                 )
 
-        spread(token_plane, token_stage)
+        width = Z // 4
+        for q in range(4):
+            src = 64 * (q // 2)
+            nc.vector.tensor_copy(
+                token_plane[32 * q : 32 * q + 4, :].bitcast(I32),
+                token_stage[src : src + 4, width * (q % 2) : width * (q % 2 + 1)],
+            )
         picked_plane = sb.tile([P, J], U8, name="picked_plane", align_bytes=64)
         nc.vector.tensor_copy(picked_plane[:], token_plane[:].indirect(token_list[:]))
         spread(w_plane, w_stage)
         spread(w2_plane, w2_stage)
+
+        make_identity(nc, identity[:])
+        turned = ps.tile([P, P], F32, name="turned")
+        nc.tensor.transpose(turned[:], weight_rows[:], identity[:])
+        nc.vector.tensor_copy(weight[:], turned[:, 0:N_TILES])
 
         z = sb.tile([P, PACK * J], BF16, name="z", align_bytes=64)
         for r in range(PACK):
@@ -114,7 +127,7 @@ def tile_list_codesbeside_kernel(tc, ca, sa, xo_words, xo_scales, w_words, w_sca
                     scale=step[:, r : r + 1],
                 )
 
-        tags = ("stage_then_codes", "picked_then_codes")
+        tags = ("codes", "picked_then_codes")
         picked = [
             sb.tile([P, HALF], U32, name="picked0", tag=tags[1], align_bytes=64),
             sb.tile([P, HALF], U32, name="picked1", align_bytes=64),
@@ -130,7 +143,7 @@ def tile_list_codesbeside_kernel(tc, ca, sa, xo_words, xo_scales, w_words, w_sca
         def code_pass(acc, t, codes, first):
             nc.tensor.matmul_mx(
                 acc[:],
-                lhsT=w_tile[t][:].bitcast(E5M2),
+                lhsT=w_tile[:, P * t : P * (t + 1)].bitcast(E5M2),
                 lhsT_scale=w_plane[:, P * t : P * (t + 1)],
                 rhs=codes[0][:].bitcast(E4M3),
                 rhs_scale=codes[1][:],
@@ -141,7 +154,7 @@ def tile_list_codesbeside_kernel(tc, ca, sa, xo_words, xo_scales, w_words, w_sca
         def token_pass(acc, t, h, first):
             nc.tensor.matmul_mx(
                 acc[:],
-                lhsT=w2_tile[t][:].bitcast(E4M3),
+                lhsT=w2_tile[:, P * t : P * (t + 1)].bitcast(E4M3),
                 lhsT_scale=w2_plane[:, P * t : P * (t + 1)],
                 rhs=picked[h][:].bitcast(E5M2),
                 rhs_scale=picked_plane[:, halves[h]],
@@ -156,7 +169,7 @@ def tile_list_codesbeside_kernel(tc, ca, sa, xo_words, xo_scales, w_words, w_sca
                 page[t][:].indirect(entries(page_list, halves[h])),
                 sums[:],
                 COPY,
-                scale=weight[t][:],
+                scale=weight[:, t : t + 1],
             )
 
         codes = quantise(0)

from contextlib import ExitStack

import concourse.mybir as mybir
from concourse.masks import make_identity

F32 = mybir.dt.float32
BF16 = mybir.dt.bfloat16
I32 = mybir.dt.int32
U32 = mybir.dt.uint32
U16 = mybir.dt.uint16
U8 = mybir.dt.uint8
E4M3 = mybir.dt.float8_e4m3fn_x4
E5M2 = mybir.dt.float8_e5m2_x4
COPY = mybir.ActivationFunctionType.Copy

P = 128
PACK = 4
K, T, F, Z, J, N, E = 512, 512, 512, 1024, 256, 256, 512
HALF = J // 2
N_TILES = N // P

FLOPS = 2 * (K + F) * N * J


def entries(list_tile, cases):
    return list_tile[:, cases.start // 16 : cases.stop // 16]


def tile_list_codesbeside_kernel(tc, ca, sa, xo_words, xo_scales, w_words, w_scales, w2_words, w2_scales, so, offs, offs2, offs3, out):
    nc = tc.nc
    halves = (slice(0, HALF), slice(HALF, J))
    every = slice(0, J)
    with ExitStack() as ctx:
        sb = ctx.enter_context(tc.tile_pool(name="sb", bufs=1))
        ps = ctx.enter_context(tc.psum_pool(name="ps", bufs=1))

        code_list = sb.tile([P, J // 16], U16, name="code_list")
        token_list = sb.tile([P, J // 16], U16, name="token_list")
        page_list = sb.tile([P, J // 16], U16, name="page_list")
        step = sb.tile([P, PACK], F32, name="step")
        weight_rows = sb.tile([P, P], F32, name="weight_rows")
        identity = sb.tile([P, P], F32, name="identity")
        weight = sb.tile([P, N_TILES], F32, name="weight")
        table = [sb.tile([P, T], F32, name="table%d" % r) for r in range(PACK)]
        tokens = sb.tile([P, Z], I32, name="tokens")
        w_tile = sb.tile([P, N], I32, name="w_tile", align_bytes=64)
        w2_tile = sb.tile([P, N], I32, name="w2_tile", align_bytes=64)
        token_stage = sb.tile([P, 2 * Z // 4], I32, name="token_stage")
        w_stage = sb.tile([4, N], I32, name="w_stage")
        w2_stage = sb.tile([4, N], I32, name="w2_stage")
        token_plane = sb.tile([P, Z], U8, name="token_plane")
        w_plane = sb.tile([P, N], U8, name="w_plane", align_bytes=64)
        w2_plane = sb.tile([P, N], U8, name="w2_plane", align_bytes=64)
        page = [sb.tile([P, E], F32, name="page%d" % t) for t in range(N_TILES)]

        ca_rows = ca.rearrange("(p r) t -> p r t", r=PACK)

        def words(src):
            return src[0].rearrange("p n b -> p (n b)").bitcast(I32)

        def scale_rows(scales):
            return scales[0].rearrange("(q r) c -> r q c", r=4).bitcast(I32)

        nc.vector.memset(weight_rows[:], 0.0)
        nc.scalar.dma_start(step[:], sa.rearrange("(p r) o -> p (r o)", r=PACK))
        for u in range(2):
            nc.sync.dma_start(
                token_stage[64 * u : 64 * u + 4, :].rearrange("r (q c) -> r q c", q=2),
                scale_rows(xo_scales)[:, 2 * u : 2 * u + 2, :],
            )
        for stage, scales in ((w_stage, w_scales), (w2_stage, w2_scales)):
            nc.sync.dma_start(stage[:].rearrange("r (q c) -> r q c", q=4), scale_rows(scales))
        nc.sync.dma_start(table[0][:], ca_rows[:, 0, :])
        nc.sync.dma_start(code_list[:], offs)
        nc.sync.dma_start(table[1][:], ca_rows[:, 1, :])
        nc.sync.dma_start(table[2][:], ca_rows[:, 2, :])
        nc.sync.dma_start(token_list[:], offs2)
        nc.sync.dma_start(table[3][:], ca_rows[:, 3, :])
        nc.sync.dma_start(weight_rows[0:N_TILES, :], so.rearrange("(t p) o -> t (p o)", p=P))
        nc.sync.dma_start(tokens[:], words(xo_words))
        nc.sync.dma_start(w_tile[:], words(w_words))
        nc.sync.dma_start(w2_tile[:], words(w2_words))
        nc.sync.dma_start(page_list[:], offs3)

        idle_in = sb.tile([P, 1], F32, name="idle_in")
        idle_out = sb.tile([P, 1], F32, name="idle_out")
        nc.vector.memset(idle_in[:], 0.0)
        nc.scalar.activation(idle_out[:], idle_in[:], COPY)

        for plane in (token_plane, w_plane, w2_plane):
            nc.vector.memset(plane[:].bitcast(I32), 0)
        for t in range(N_TILES):
            nc.vector.memset(page[t][:], 0.0)

        def spread(plane, stage):
            width = stage.shape[1] // 4
            for q in range(4):
                nc.vector.tensor_copy(
                    plane[32 * q : 32 * q + 4, :].bitcast(I32),
                    stage[0:4, width * q : width * (q + 1)],
                )

        width = Z // 4
        for q in range(4):
            src = 64 * (q // 2)
            nc.vector.tensor_copy(
                token_plane[32 * q : 32 * q + 4, :].bitcast(I32),
                token_stage[src : src + 4, width * (q % 2) : width * (q % 2 + 1)],
            )
        picked_plane = sb.tile([P, J], U8, name="picked_plane", align_bytes=64)
        nc.vector.tensor_copy(picked_plane[:], token_plane[:].indirect(token_list[:]))
        spread(w_plane, w_stage)
        spread(w2_plane, w2_stage)

        make_identity(nc, identity[:])
        turned = ps.tile([P, P], F32, name="turned")
        nc.tensor.transpose(turned[:], weight_rows[:], identity[:])
        nc.vector.tensor_copy(weight[:], turned[:, 0:N_TILES])

        z = sb.tile([P, PACK * J], BF16, name="z", align_bytes=64)
        for r in range(PACK):
            for cases in halves if r == PACK - 1 else (every,):
                nc.scalar.activation(
                    z[:, PACK * cases.start + r : PACK * cases.stop : PACK],
                    table[r][:].indirect(entries(code_list, cases)),
                    COPY,
                    scale=step[:, r : r + 1],
                )

        tags = ("codes", "picked_then_codes")
        picked = [
            sb.tile([P, HALF], U32, name="picked0", tag=tags[1], align_bytes=64),
            sb.tile([P, HALF], U32, name="picked1", align_bytes=64),
        ]

        def quantise(h):
            z_words = sb.tile([P, HALF], U32, name="z_words%d" % h, tag=tags[h], align_bytes=64)
            z_plane = sb.tile([P, HALF], U8, name="z_plane%d" % h, align_bytes=64)
            cases = halves[h]
            nc.vector.quantize_mx(z_words[:].bitcast(E4M3), z_plane[:], z[:, PACK * cases.start : PACK * cases.stop])
            return z_words, z_plane

        def code_pass(acc, t, codes, first):
            nc.tensor.matmul_mx(
                acc[:],
                lhsT=w_tile[:, P * t : P * (t + 1)].bitcast(E5M2),
                lhsT_scale=w_plane[:, P * t : P * (t + 1)],
                rhs=codes[0][:].bitcast(E4M3),
                rhs_scale=codes[1][:],
                start=first,
                stop=not first,
            )

        def token_pass(acc, t, h, first):
            nc.tensor.matmul_mx(
                acc[:],
                lhsT=w2_tile[:, P * t : P * (t + 1)].bitcast(E4M3),
                lhsT_scale=w2_plane[:, P * t : P * (t + 1)],
                rhs=picked[h][:].bitcast(E5M2),
                rhs_scale=picked_plane[:, halves[h]],
                start=first,
                stop=not first,
            )

        def put(acc, t, h):
            sums = sb.tile([P, HALF], F32, name="sums%d%d" % (t, h))
            nc.vector.tensor_copy(sums[:], acc[:])
            nc.scalar.activation(
                page[t][:].indirect(entries(page_list, halves[h])),
                sums[:],
                COPY,
                scale=weight[:, t : t + 1],
            )

        codes = quantise(0)
        for h in range(2):
            nc.vector.tensor_copy(picked[h][:], tokens[:].bitcast(U32).indirect(entries(token_list, halves[h])))
        for t in range(N_TILES):
            acc = ps.tile([P, HALF], F32, name="acc%d0" % t)
            code_pass(acc, t, codes, True)
            token_pass(acc, t, 0, False)
            put(acc, t, 0)
        codes = quantise(1)
        for t in range(N_TILES):
            acc = ps.tile([P, HALF], F32, name="acc%d1" % t)
            token_pass(acc, t, 1, True)
            code_pass(acc, t, codes, False)
            put(acc, t, 1)
        for t in range(N_TILES):
            nc.sync.dma_start(out[P * t : P * (t + 1), :], page[t][:])
